import numpy as np
import ml_dtypes


def mxq(x, axis, fmt="e4m3"):
    dtype, down = {"e4m3": (ml_dtypes.float8_e4m3fn, 7), "e5m2": (ml_dtypes.float8_e5m2, 14)}[fmt]
    v = np.moveaxis(np.asarray(x, np.float32).astype(ml_dtypes.bfloat16).astype(np.float64), axis, -1)
    blocks = v.reshape(v.shape[:-1] + (-1, 32))
    amax = np.abs(blocks).max(-1, keepdims=True)
    byte = np.maximum(np.where(amax > 0, np.frexp(amax)[1] - 1 + 127, 0) - down, 1)
    scale = np.exp2(byte - 127.0)
    codes = (blocks / scale).astype(np.float32).astype(dtype).astype(np.float64)
    return np.moveaxis((codes * scale).reshape(v.shape), -1, axis)


WIDE = False


def mx_kscale(k):
    if not WIDE:
        return np.ones(k)
    levels = np.array([30, -30])
    if k % 512:
        return np.exp2(np.random.permutation(np.resize(levels, k // 32))).repeat(32)
    a = np.empty((k // 512, 16))
    for p in range(k // 512):
        a[p, :8] = np.random.permutation(np.resize(levels, 8))
        for g in range(8):
            far = levels[np.abs(levels - a[p, g]) >= 10]
            a[p, g + 8] = far[np.random.randint(len(far))]
    return np.exp2(a.ravel()).repeat(32)


def f64(x):
    return np.asarray(x).astype(np.float64)


def striped(idx):
    return np.tile(np.asarray(idx).reshape(-1, 16).T, (8, 1)).astype(np.uint16)


def unstriped(offs):
    return offs[:16].T.reshape(-1).astype(np.int64)


E2M1 = np.array([0.0, 0.5, 1.0, 1.5, 2.0, 3.0, 4.0, 6.0, -0.0, -0.5, -1.0, -1.5, -2.0, -3.0, -4.0, -6.0])


def pack_weight(w, fmt):
    k, n = w.shape
    w = f64(np.asarray(w, np.float32).astype(ml_dtypes.bfloat16)).reshape(k // 32, 32, n)
    amax = np.abs(w).max(1)
    if fmt == "e4m3":
        byte = np.frexp(amax)[1] - 1 + 127 - 7
    else:
        mant, ex = np.frexp(amax / 6.0)
        byte = np.where(mant > 0.5, ex, ex - 1) + 127
    byte = np.clip(np.where(amax > 0, byte, 1), 1, 254)
    scaled = (w * np.exp2(127.0 - byte)[:, None, :]).reshape(k, n).astype(np.float32)
    by_word = np.ascontiguousarray(scaled.reshape(k // 512, 128, 4, n).transpose(0, 1, 3, 2))
    if fmt == "e4m3":
        words = by_word.astype(ml_dtypes.float8_e4m3fn).view(np.uint8)
    else:
        c = by_word.astype(ml_dtypes.float4_e2m1fn).view(np.uint8) & 0xF
        words = (c[..., 0::2] | (c[..., 1::2] << 4)).reshape(k // 512, 128, 2 * n)
    return np.ascontiguousarray(words), np.ascontiguousarray(byte.astype(np.uint8).reshape(k // 512, 16, n))


def unpack_weight(words, scales, fmt):
    g, _, n = scales.shape
    words = np.ascontiguousarray(words).reshape(g, 128, n, -1)
    if fmt == "e4m3":
        vals = words.view(ml_dtypes.float8_e4m3fn).astype(np.float64)
    else:
        nib = np.empty((g, 128, n, 4), np.uint8)
        nib[..., 0::2] = words & 0xF
        nib[..., 1::2] = words >> 4
        vals = E2M1[nib]
    vals = vals * np.repeat(np.exp2(scales.astype(np.float64) - 127.0), 8, axis=1)[..., None]
    return vals.transpose(0, 1, 3, 2).reshape(g * 512, n)


def sigmoid(v):
    return 1.0 / (1.0 + np.exp(-v))


K, F, T, Z, J, R, O, N, E = 512, 512, 1024, 1024, 256, 512, 128, 256, 512


def setup_inputs():
    n = np.random.standard_normal
    idx = np.random.permutation(T)[:J]
    idx2 = np.random.permutation(Z)[:J]
    idx3 = np.random.permutation(J)[:O]
    idx4 = np.random.permutation(J)[:O]
    idx5 = np.random.permutation(E)[:O]
    fk = mx_kscale(K)
    ff = mx_kscale(F)
    fr = mx_kscale(R)
    xtp = pack_weight(n((K, T)) / fk[:, None], "e2m1")
    wp = pack_weight(n((K, R)) * 1 / np.sqrt(K) * fk[:, None], "e4m3")
    xop = pack_weight(n((F, Z)) / ff[:, None], "e4m3")
    w2p = pack_weight(n((F, R)) * 1 / np.sqrt(F) * ff[:, None] * fr, "e2m1")
    wbp = pack_weight(n((R, N)) * 1 / np.sqrt(R) / fr[:, None], "e2m1")
    return {
        "xt_words": xtp[0],
        "xt_scales": xtp[1],
        "w_words": wp[0],
        "w_scales": wp[1],
        "xo_words": xop[0],
        "xo_scales": xop[1],
        "w2_words": w2p[0],
        "w2_scales": w2p[1],
        "sg": (np.random.uniform(0.6, 1.6, (R, 1))).astype(np.float32),
        "bg": (np.random.uniform(-1.0, 1.0, (R, 1))).astype(np.float32),
        "wb_words": wbp[0],
        "wb_scales": wbp[1],
        "tz": (n((N, E))).astype(np.float32),
        "so": (np.random.uniform(0.6, 1.6, (N, 1))).astype(np.float32),
        "bo": (np.random.uniform(-1.0, 1.0, (N, 1))).astype(np.float32),
        "offs": striped(idx),
        "offs2": striped(idx2),
        "offs3": striped(idx3),
        "offs4": striped(idx4),
        "offs5": striped(idx5),
    }


def reference(xt_words, xt_scales, w_words, w_scales, xo_words, xo_scales, w2_words, w2_scales, sg, bg, wb_words, wb_scales, tz, so, bo, offs, offs2, offs3, offs4, offs5):
    idx = unstriped(offs)
    idx2 = unstriped(offs2)
    idx3 = unstriped(offs3)
    idx4 = unstriped(offs4)
    idx5 = unstriped(offs5)
    xtu = unpack_weight(xt_words, xt_scales, "e2m1")
    wu = unpack_weight(w_words, w_scales, "e4m3")
    xou = unpack_weight(xo_words, xo_scales, "e4m3")
    w2u = unpack_weight(w2_words, w2_scales, "e2m1")
    wbu = unpack_weight(wb_words, wb_scales, "e2m1")
    xtidxg = xtu[:, idx]
    a = wu.T @ xtidxg
    xoidx2g = xou[:, idx2]
    b = w2u.T @ xoidx2g
    hid = b[:, idx4] * sigmoid(a[:, idx3] * f64(sg) + f64(bg))
    hidq = mxq(hid, 0, "e5m2")
    p = wbu.T @ hidq
    y = p * sigmoid(f64(tz)[:, idx5] * f64(so) + f64(bo))
    return y

@@ -1,0 +1,145 @@
+from contextlib import ExitStack
+
+import concourse.mybir as mybir
+
+F32 = mybir.dt.float32
+BF16 = mybir.dt.bfloat16
+I32 = mybir.dt.int32
+U32 = mybir.dt.uint32
+U16 = mybir.dt.uint16
+U8 = mybir.dt.uint8
+E4M3X4 = mybir.dt.float8_e4m3fn_x4
+E5M2X4 = mybir.dt.float8_e5m2_x4
+E2M1X4 = mybir.dt.float4_e2m1fn_x4
+SIGMOID = mybir.ActivationFunctionType.Sigmoid
+COPY = mybir.ActivationFunctionType.Copy
+MULT = mybir.AluOpType.mult
+
+P = 128
+PACK = 4
+K, F, T, Z, J, R, O, N, E = 512, 512, 1024, 1024, 256, 512, 128, 256, 512
+FLOPS = 2 * K * R * J + 2 * F * R * J + 2 * R * N * O
+
+
+def load_scale_rows(queue, plane, scales):
+    for q in range(4):
+        queue.dma_start(out=plane[32 * q : 32 * q + 4, :].bitcast(I32), in_=scales[0, 4 * q : 4 * q + 4, :].bitcast(I32))
+
+
+def deal_columns(copy, dst, src):
+    copy(out=dst.rearrange("p (t m) -> p m t", t=PACK), in_=src.rearrange("p (m t) -> p m t", t=PACK))
+
+
+def tile_list_twotab_gatefetch_one_finalgate_kernel(
+    tc, xt_words, xt_scales, w_words, w_scales, xo_words, xo_scales, w2_words, w2_scales, sg, bg,
+    wb_words, wb_scales, tz, so, bo, offs, offs2, offs3, offs4, offs5, out,
+):
+    nc = tc.nc
+    with ExitStack() as ctx:
+        keep = ctx.enter_context(tc.tile_pool(name="keep", bufs=1))
+        psum = ctx.enter_context(tc.psum_pool(name="psum", bufs=4))
+
+        def sb(name, cols, dtype, tag=None):
+            return keep.tile([P, cols], dtype, name=name, tag=tag or name, align_bytes=64)
+
+        l1, l2 = sb("l1", J // 16, U16), sb("l2", J // 16, U16)
+        l3, l4, l5 = sb("l3", O // 16, U16), sb("l4", O // 16, U16), sb("l5", O // 16, U16)
+        xt_w, xt_s = sb("xt_w", T, U16), sb("xt_s", T, U8)
+        xo_w, xo_s = sb("xo_w", Z, U32), sb("xo_s", Z, U8)
+        w_w, w_s = sb("w_w", R, U32), sb("w_s", R, U8)
+        w2_w, w2_s = sb("w2_w", R, U16), sb("w2_s", R, U8)
+        wb_w, wb_s = sb("wb_w", 2 * N, U8), sb("wb_s", N, U8)
+        sg_t, bg_t = sb("sg_t", PACK, F32), sb("bg_t", PACK, F32)
+        so_t, bo_t = sb("so_t", 2, F32), sb("bo_t", 2, F32)
+
+        nc.gpsimd.memset(xt_s[:].bitcast(I32), 0)
+        nc.vector.memset(w_s[:].bitcast(I32), 0)
+        nc.vector.memset(xo_s[:].bitcast(I32), 0)
+        nc.vector.memset(w2_s[:].bitcast(I32), 0)
+        nc.vector.memset(wb_s[:].bitcast(I32), 0)
+
+        nc.sync.dma_start(out=xt_w[:].bitcast(I32), in_=xt_words[0].bitcast(I32))
+        nc.sync.dma_start(out=l1[:], in_=offs)
+        load_scale_rows(nc.sync, xt_s, xt_scales)
+        nc.sync.dma_start(out=w_w[:].bitcast(I32), in_=w_words[0].rearrange("p n t -> p (n t)").bitcast(I32))
+        load_scale_rows(nc.sync, w_s, w_scales)
+        nc.sync.dma_start(out=l2[:], in_=offs2)
+        nc.sync.dma_start(out=xo_w[:].bitcast(I32), in_=xo_words[0].rearrange("p n t -> p (n t)").bitcast(I32))
+        load_scale_rows(nc.sync, xo_s, xo_scales)
+        nc.sync.dma_start(out=w2_w[:].bitcast(I32), in_=w2_words[0].bitcast(I32))
+        load_scale_rows(nc.sync, w2_s, w2_scales)
+        nc.sync.dma_start(out=l3[:], in_=offs3)
+        nc.sync.dma_start(out=l4[:], in_=offs4)
+        nc.sync.dma_start(out=l5[:], in_=offs5)
+        nc.sync.dma_start(out=wb_w[:].bitcast(I32), in_=wb_words[0].bitcast(I32))
+        nc.gpsimd.dma_start(out=sg_t[:], in_=sg.rearrange("(p t) o -> p (t o)", t=PACK))
+        nc.gpsimd.dma_start(out=bg_t[:], in_=bg.rearrange("(p t) o -> p (t o)", t=PACK))
+        with nc.allow_non_contiguous_dma(reason="one value a partition and half"):
+            nc.gpsimd.dma_start(out=so_t[:], in_=so.rearrange("(h p) o -> p (h o)", p=P))
+            nc.gpsimd.dma_start(out=bo_t[:], in_=bo.rearrange("(h p) o -> p (h o)", p=P))
+        load_scale_rows(nc.sync, wb_s, wb_scales)
+
+        xt_gw, xt_gs = sb("xt_gw", J, U16), sb("xt_gs", J, U8)
+        xo_gw, xo_gs = sb("xo_gw", J, U32), sb("xo_gs", J, U8)
+        w_dw, w_ds = sb("w_dw", R, U32), sb("w_ds", R, U8)
+        w2_dw, w2_ds = sb("w2_dw", R, U16), sb("w2_ds", R, U8)
+
+        nc.vector.tensor_copy(out=xt_gw[:], in_=xt_w[:].indirect(l1[:]))
+        nc.vector.tensor_copy(out=xt_gs[:], in_=xt_s[:].indirect(l1[:]))
+        deal_columns(nc.scalar.copy, w_dw[:], w_w[:])
+        deal_columns(nc.vector.tensor_copy, w_ds[:], w_s[:])
+        nc.vector.tensor_copy(out=xo_gw[:], in_=xo_w[:].indirect(l2[:]))
+        nc.vector.tensor_copy(out=xo_gs[:], in_=xo_s[:].indirect(l2[:]))
+        deal_columns(nc.scalar.copy, w2_dw[:], w2_w[:])
+        deal_columns(nc.vector.tensor_copy, w2_ds[:], w2_s[:])
+
+        tz_t = [sb("tz0", E, F32, tag="xt_w"), sb("tz1", E, F32, tag="w_w")]
+        for h in range(2):
+            nc.sync.dma_start(out=tz_t[h][:], in_=tz[h * P : (h + 1) * P, :])
+
+        gate = keep.tile([P, PACK, O], F32, name="gate", align_bytes=64)
+        b_pick = keep.tile([P, PACK, O], F32, name="b_pick", align_bytes=64)
+        for t in range(PACK):
+            cols = slice(t * P, (t + 1) * P)
+            a_ps = psum.tile([P, J], F32, name="a_ps", tag="a")
+            nc.tensor.matmul_mx(out=a_ps[:], lhsT=w_dw[:, cols].bitcast(E4M3X4), lhsT_scale=w_ds[:, cols],
+                                rhs=xt_gw[:].bitcast(E2M1X4), rhs_scale=xt_gs[:], start=True, stop=True)
+            a_sb = sb(f"a_sb{t}", J, F32)
+            nc.scalar.copy(out=a_sb[:], in_=a_ps[:])
+            nc.scalar.activation(out=gate[:, t, :], in_=a_sb[:].indirect(l3[:]), func=SIGMOID,
+                                 bias=bg_t[:, t : t + 1], scale=sg_t[:, t : t + 1])
+        for t in range(PACK):
+            cols = slice(t * P, (t + 1) * P)
+            b_ps = psum.tile([P, J], F32, name="b_ps", tag="b")
+            nc.tensor.matmul_mx(out=b_ps[:], lhsT=w2_dw[:, cols].bitcast(E2M1X4), lhsT_scale=w2_ds[:, cols],
+                                rhs=xo_gw[:].bitcast(E4M3X4), rhs_scale=xo_gs[:], start=True, stop=True)
+            b_sb = sb(f"b_sb{t}", J, F32)
+            if t < PACK - 1:
+                nc.vector.tensor_copy(out=b_sb[:], in_=b_ps[:])
+                nc.vector.tensor_copy(out=b_pick[:, t, :], in_=b_sb[:].indirect(l4[:]))
+            else:
+                nc.scalar.copy(out=b_sb[:], in_=b_ps[:])
+                nc.scalar.activation(out=b_pick[:, t, :], in_=b_sb[:].indirect(l4[:]), func=COPY)
+
+        hid = sb("hid", PACK * O, BF16)
+        nc.vector.tensor_tensor(
+            out=hid[:].rearrange("p (g i t) -> p g t i", t=PACK, i=4),
+            in0=b_pick[:].rearrange("p t (g i) -> p g t i", i=4),
+            in1=gate[:].rearrange("p t (g i) -> p g t i", i=4),
+            op=MULT,
+        )
+        hid_w, hid_s = sb("hid_w", O, U32), sb("hid_s", O, U8)
+        nc.vector.quantize_mx(out=hid_w[:].bitcast(E5M2X4), scales=hid_s[:], in_=hid[:])
+
+        last = sb("last", 2 * O, F32, tag="b_sb3")
+        for h in range(2):
+            nc.scalar.activation(out=last[:, h * O : (h + 1) * O], in_=tz_t[h][:].indirect(l5[:]), func=SIGMOID,
+                                 bias=bo_t[:, h : h + 1], scale=so_t[:, h : h + 1])
+            p_ps = psum.tile([P, O], F32, name="p_ps", tag="a")
+            nc.tensor.matmul_mx(out=p_ps[:], lhsT=wb_w[:, 2 * h * P : 2 * (h + 1) * P].bitcast(E2M1X4),
+                                lhsT_scale=wb_s[:, h * P : (h + 1) * P],
+                                rhs=hid_w[:].bitcast(E5M2X4), rhs_scale=hid_s[:], start=True, stop=True)
+            res = sb(f"res{h}", O, F32)
+            nc.vector.tensor_tensor(out=res[:], in0=p_ps[:], in1=last[:, h * O : (h + 1) * O], op=MULT)
+            queue = nc.sync if h == 0 else nc.scalar
+            queue.dma_start(out=out[h * P : (h + 1) * P, :], in_=res[:])

@@ -58,6 +58,10 @@ def tile_list_twotab_gatefetch_one_finalgate_kernel(
         nc.vector.memset(w2_s[:].bitcast(I32), 0)
         nc.vector.memset(wb_s[:].bitcast(I32), 0)
 
+        warm_in, warm_out = sb("warm_in", 1, F32), sb("warm_out", 1, F32)
+        nc.vector.memset(warm_in[:], 0.0)
+        nc.scalar.activation(out=warm_out[:], in_=warm_in[:], func=SIGMOID)
+
         nc.sync.dma_start(out=xt_w[:].bitcast(I32), in_=xt_words[0].bitcast(I32))
         nc.sync.dma_start(out=l1[:], in_=offs)
         load_scale_rows(nc.sync, xt_s, xt_scales)

@@ -66,40 +66,37 @@ def tile_list_twotab_gatefetch_one_finalgate_kernel(
         nc.sync.dma_start(out=l1[:], in_=offs)
         load_scale_rows(nc.sync, xt_s, xt_scales)
         nc.sync.dma_start(out=w_w[:].bitcast(I32), in_=w_words[0].rearrange("p n t -> p (n t)").bitcast(I32))
-        load_scale_rows(nc.sync, w_s, w_scales)
-        nc.sync.dma_start(out=l2[:], in_=offs2)
         nc.sync.dma_start(out=xo_w[:].bitcast(I32), in_=xo_words[0].rearrange("p n t -> p (n t)").bitcast(I32))
-        load_scale_rows(nc.sync, xo_s, xo_scales)
+        load_scale_rows(nc.sync, w_s, w_scales)
         nc.sync.dma_start(out=w2_w[:].bitcast(I32), in_=w2_words[0].bitcast(I32))
-        load_scale_rows(nc.sync, w2_s, w2_scales)
+        nc.sync.dma_start(out=l2[:], in_=offs2)
         nc.sync.dma_start(out=l3[:], in_=offs3)
+        load_scale_rows(nc.sync, xo_s, xo_scales)
+        load_scale_rows(nc.sync, w2_s, w2_scales)
         nc.sync.dma_start(out=l4[:], in_=offs4)
         nc.sync.dma_start(out=l5[:], in_=offs5)
+        with nc.allow_non_contiguous_dma(reason="one value a partition and half"):
+            nc.sync.dma_start(out=so_t[:], in_=so.rearrange("(h p) o -> p (h o)", p=P))
+            nc.sync.dma_start(out=bo_t[:], in_=bo.rearrange("(h p) o -> p (h o)", p=P))
+        tz_t = [sb(f"tz{h}", E, F32) for h in range(2)]
+        for h in range(2):
+            nc.sync.dma_start(out=tz_t[h][:], in_=tz[h * P : (h + 1) * P, :])
+        load_scale_rows(nc.sync, wb_s, wb_scales)
         nc.sync.dma_start(out=wb_w[:].bitcast(I32), in_=wb_words[0].bitcast(I32))
         nc.gpsimd.dma_start(out=sg_t[:], in_=sg.rearrange("(p t) o -> p (t o)", t=PACK))
         nc.gpsimd.dma_start(out=bg_t[:], in_=bg.rearrange("(p t) o -> p (t o)", t=PACK))
-        with nc.allow_non_contiguous_dma(reason="one value a partition and half"):
-            nc.gpsimd.dma_start(out=so_t[:], in_=so.rearrange("(h p) o -> p (h o)", p=P))
-            nc.gpsimd.dma_start(out=bo_t[:], in_=bo.rearrange("(h p) o -> p (h o)", p=P))
-        load_scale_rows(nc.sync, wb_s, wb_scales)
 
         xt_gw, xt_gs = sb("xt_gw", J, U16), sb("xt_gs", J, U8)
-        xo_gw, xo_gs = sb("xo_gw", J, U32), sb("xo_gs", J, U8)
         w_dw, w_ds = sb("w_dw", R, U32), sb("w_ds", R, U8)
-        w2_dw, w2_ds = sb("w2_dw", R, U16), sb("w2_ds", R, U8)
+        w2_dw = sb("w2_dw", R, U16)
 
         nc.vector.tensor_copy(out=xt_gw[:], in_=xt_w[:].indirect(l1[:]))
         nc.vector.tensor_copy(out=xt_gs[:], in_=xt_s[:].indirect(l1[:]))
         deal_columns(nc.scalar.copy, w_dw[:], w_w[:])
         deal_columns(nc.vector.tensor_copy, w_ds[:], w_s[:])
-        nc.vector.tensor_copy(out=xo_gw[:], in_=xo_w[:].indirect(l2[:]))
-        nc.vector.tensor_copy(out=xo_gs[:], in_=xo_s[:].indirect(l2[:]))
         deal_columns(nc.scalar.copy, w2_dw[:], w2_w[:])
-        deal_columns(nc.vector.tensor_copy, w2_ds[:], w2_s[:])
-
-        tz_t = [sb("tz0", E, F32, tag="xt_w"), sb("tz1", E, F32, tag="w_w")]
-        for h in range(2):
-            nc.sync.dma_start(out=tz_t[h][:], in_=tz[h * P : (h + 1) * P, :])
+        xo_gw = sb("xo_gw", J, U32, tag="w_s")
+        nc.vector.tensor_copy(out=xo_gw[:], in_=xo_w[:].indirect(l2[:]))
 
         gate = keep.tile([P, PACK, O], F32, name="gate", align_bytes=64)
         b_pick = keep.tile([P, PACK, O], F32, name="b_pick", align_bytes=64)
@@ -112,18 +109,23 @@ def tile_list_twotab_gatefetch_one_finalgate_kernel(
             nc.scalar.copy(out=a_sb[:], in_=a_ps[:])
             nc.scalar.activation(out=gate[:, t, :], in_=a_sb[:].indirect(l3[:]), func=SIGMOID,
                                  bias=bg_t[:, t : t + 1], scale=sg_t[:, t : t + 1])
+
+        xo_gs, w2_ds = sb("xo_gs", J, U8), sb("w2_ds", R, U8)
+        nc.vector.tensor_copy(out=xo_gs[:], in_=xo_s[:].indirect(l2[:]))
+        deal_columns(nc.vector.tensor_copy, w2_ds[:], w2_s[:])
+        b_sb = [sb(f"b_sb{t}", J, F32) for t in range(PACK)]
         for t in range(PACK):
             cols = slice(t * P, (t + 1) * P)
             b_ps = psum.tile([P, J], F32, name="b_ps", tag="b")
             nc.tensor.matmul_mx(out=b_ps[:], lhsT=w2_dw[:, cols].bitcast(E2M1X4), lhsT_scale=w2_ds[:, cols],
                                 rhs=xo_gw[:].bitcast(E4M3X4), rhs_scale=xo_gs[:], start=True, stop=True)
-            b_sb = sb(f"b_sb{t}", J, F32)
-            if t < PACK - 1:
-                nc.vector.tensor_copy(out=b_sb[:], in_=b_ps[:])
-                nc.vector.tensor_copy(out=b_pick[:, t, :], in_=b_sb[:].indirect(l4[:]))
+            copy = nc.vector.tensor_copy if t < 2 else nc.scalar.copy
+            copy(out=b_sb[t][:], in_=b_ps[:])
+        for t in range(PACK):
+            if t != 2:
+                nc.vector.tensor_copy(out=b_pick[:, t, :], in_=b_sb[t][:].indirect(l4[:]))
             else:
-                nc.scalar.copy(out=b_sb[:], in_=b_ps[:])
-                nc.scalar.activation(out=b_pick[:, t, :], in_=b_sb[:].indirect(l4[:]), func=COPY)
+                nc.scalar.activation(out=b_pick[:, t, :], in_=b_sb[t][:].indirect(l4[:]), func=COPY)
 
         hid = sb("hid", PACK * O, BF16)
         nc.vector.tensor_tensor(
@@ -135,7 +137,7 @@ def tile_list_twotab_gatefetch_one_finalgate_kernel(
         hid_w, hid_s = sb("hid_w", O, U32), sb("hid_s", O, U8)
         nc.vector.quantize_mx(out=hid_w[:].bitcast(E5M2X4), scales=hid_s[:], in_=hid[:])
 
-        last = sb("last", 2 * O, F32, tag="b_sb3")
+        last = sb("last", 2 * O, F32, tag="b_sb2")
         for h in range(2):
             nc.scalar.activation(out=last[:, h * O : (h + 1) * O], in_=tz_t[h][:].indirect(l5[:]), func=SIGMOID,
                                  bias=bo_t[:, h : h + 1], scale=so_t[:, h : h + 1])

from contextlib import ExitStack

import concourse.mybir as mybir

F32 = mybir.dt.float32
BF16 = mybir.dt.bfloat16
I32 = mybir.dt.int32
U32 = mybir.dt.uint32
U16 = mybir.dt.uint16
U8 = mybir.dt.uint8
E4M3X4 = mybir.dt.float8_e4m3fn_x4
E5M2X4 = mybir.dt.float8_e5m2_x4
E2M1X4 = mybir.dt.float4_e2m1fn_x4
SIGMOID = mybir.ActivationFunctionType.Sigmoid
COPY = mybir.ActivationFunctionType.Copy
MULT = mybir.AluOpType.mult

P = 128
PACK = 4
K, F, T, Z, J, R, O, N, E = 512, 512, 1024, 1024, 256, 512, 128, 256, 512
FLOPS = 2 * K * R * J + 2 * F * R * J + 2 * R * N * O


def load_scale_rows(queue, plane, scales):
    for q in range(4):
        queue.dma_start(out=plane[32 * q : 32 * q + 4, :].bitcast(I32), in_=scales[0, 4 * q : 4 * q + 4, :].bitcast(I32))


def deal_columns(copy, dst, src):
    copy(out=dst.rearrange("p (t m) -> p m t", t=PACK), in_=src.rearrange("p (m t) -> p m t", t=PACK))


def tile_list_twotab_gatefetch_one_finalgate_kernel(
    tc, xt_words, xt_scales, w_words, w_scales, xo_words, xo_scales, w2_words, w2_scales, sg, bg,
    wb_words, wb_scales, tz, so, bo, offs, offs2, offs3, offs4, offs5, out,
):
    nc = tc.nc
    with ExitStack() as ctx:
        keep = ctx.enter_context(tc.tile_pool(name="keep", bufs=1))
        psum = ctx.enter_context(tc.psum_pool(name="psum", bufs=4))

        def sb(name, cols, dtype, tag=None):
            return keep.tile([P, cols], dtype, name=name, tag=tag or name, align_bytes=64)

        l1, l2 = sb("l1", J // 16, U16), sb("l2", J // 16, U16)
        l3, l4, l5 = sb("l3", O // 16, U16), sb("l4", O // 16, U16), sb("l5", O // 16, U16)
        xt_w, xt_s = sb("xt_w", T, U16), sb("xt_s", T, U8)
        xo_w, xo_s = sb("xo_w", Z, U32), sb("xo_s", Z, U8)
        w_w, w_s = sb("w_w", R, U32), sb("w_s", R, U8)
        w2_w, w2_s = sb("w2_w", R, U16), sb("w2_s", R, U8)
        wb_w, wb_s = sb("wb_w", 2 * N, U8), sb("wb_s", N, U8)
        sg_t, bg_t = sb("sg_t", PACK, F32), sb("bg_t", PACK, F32)
        so_t, bo_t = sb("so_t", 2, F32), sb("bo_t", 2, F32)

        nc.gpsimd.memset(xt_s[:].bitcast(I32), 0)
        nc.vector.memset(w_s[:].bitcast(I32), 0)
        nc.vector.memset(xo_s[:].bitcast(I32), 0)
        nc.vector.memset(w2_s[:].bitcast(I32), 0)
        nc.vector.memset(wb_s[:].bitcast(I32), 0)

        warm_in, warm_out = sb("warm_in", 1, F32), sb("warm_out", 1, F32)
        nc.vector.memset(warm_in[:], 0.0)
        nc.scalar.activation(out=warm_out[:], in_=warm_in[:], func=SIGMOID)

        nc.sync.dma_start(out=xt_w[:].bitcast(I32), in_=xt_words[0].bitcast(I32))
        nc.sync.dma_start(out=l1[:], in_=offs)
        load_scale_rows(nc.sync, xt_s, xt_scales)
        nc.sync.dma_start(out=w_w[:].bitcast(I32), in_=w_words[0].rearrange("p n t -> p (n t)").bitcast(I32))
        nc.sync.dma_start(out=xo_w[:].bitcast(I32), in_=xo_words[0].rearrange("p n t -> p (n t)").bitcast(I32))
        load_scale_rows(nc.sync, w_s, w_scales)
        nc.sync.dma_start(out=w2_w[:].bitcast(I32), in_=w2_words[0].bitcast(I32))
        nc.sync.dma_start(out=l2[:], in_=offs2)
        nc.sync.dma_start(out=l3[:], in_=offs3)
        load_scale_rows(nc.sync, xo_s, xo_scales)
        load_scale_rows(nc.sync, w2_s, w2_scales)
        nc.sync.dma_start(out=l4[:], in_=offs4)
        nc.sync.dma_start(out=l5[:], in_=offs5)
        with nc.allow_non_contiguous_dma(reason="one value a partition and half"):
            nc.sync.dma_start(out=so_t[:], in_=so.rearrange("(h p) o -> p (h o)", p=P))
            nc.sync.dma_start(out=bo_t[:], in_=bo.rearrange("(h p) o -> p (h o)", p=P))
        tz_t = [sb(f"tz{h}", E, F32) for h in range(2)]
        for h in range(2):
            nc.sync.dma_start(out=tz_t[h][:], in_=tz[h * P : (h + 1) * P, :])
        load_scale_rows(nc.sync, wb_s, wb_scales)
        nc.sync.dma_start(out=wb_w[:].bitcast(I32), in_=wb_words[0].bitcast(I32))
        nc.gpsimd.dma_start(out=sg_t[:], in_=sg.rearrange("(p t) o -> p (t o)", t=PACK))
        nc.gpsimd.dma_start(out=bg_t[:], in_=bg.rearrange("(p t) o -> p (t o)", t=PACK))

        xt_gw, xt_gs = sb("xt_gw", J, U16), sb("xt_gs", J, U8)
        w_dw, w_ds = sb("w_dw", R, U32), sb("w_ds", R, U8)
        w2_dw = sb("w2_dw", R, U16)

        nc.vector.tensor_copy(out=xt_gw[:], in_=xt_w[:].indirect(l1[:]))
        nc.vector.tensor_copy(out=xt_gs[:], in_=xt_s[:].indirect(l1[:]))
        deal_columns(nc.scalar.copy, w_dw[:], w_w[:])
        deal_columns(nc.vector.tensor_copy, w_ds[:], w_s[:])
        deal_columns(nc.scalar.copy, w2_dw[:], w2_w[:])
        xo_gw = sb("xo_gw", J, U32, tag="w_s")
        nc.vector.tensor_copy(out=xo_gw[:], in_=xo_w[:].indirect(l2[:]))

        gate = keep.tile([P, PACK, O], F32, name="gate", align_bytes=64)
        b_pick = keep.tile([P, PACK, O], F32, name="b_pick", align_bytes=64)
        for t in range(PACK):
            cols = slice(t * P, (t + 1) * P)
            a_ps = psum.tile([P, J], F32, name="a_ps", tag="a")
            nc.tensor.matmul_mx(out=a_ps[:], lhsT=w_dw[:, cols].bitcast(E4M3X4), lhsT_scale=w_ds[:, cols],
                                rhs=xt_gw[:].bitcast(E2M1X4), rhs_scale=xt_gs[:], start=True, stop=True)
            a_sb = sb(f"a_sb{t}", J, F32)
            nc.scalar.copy(out=a_sb[:], in_=a_ps[:])
            nc.scalar.activation(out=gate[:, t, :], in_=a_sb[:].indirect(l3[:]), func=SIGMOID,
                                 bias=bg_t[:, t : t + 1], scale=sg_t[:, t : t + 1])

        xo_gs, w2_ds = sb("xo_gs", J, U8), sb("w2_ds", R, U8)
        nc.vector.tensor_copy(out=xo_gs[:], in_=xo_s[:].indirect(l2[:]))
        deal_columns(nc.vector.tensor_copy, w2_ds[:], w2_s[:])
        b_sb = [sb(f"b_sb{t}", J, F32) for t in range(PACK)]
        for t in range(PACK):
            cols = slice(t * P, (t + 1) * P)
            b_ps = psum.tile([P, J], F32, name="b_ps", tag="b")
            nc.tensor.matmul_mx(out=b_ps[:], lhsT=w2_dw[:, cols].bitcast(E2M1X4), lhsT_scale=w2_ds[:, cols],
                                rhs=xo_gw[:].bitcast(E4M3X4), rhs_scale=xo_gs[:], start=True, stop=True)
            copy = nc.vector.tensor_copy if t < 2 else nc.scalar.copy
            copy(out=b_sb[t][:], in_=b_ps[:])
        for t in range(PACK):
            if t != 2:
                nc.vector.tensor_copy(out=b_pick[:, t, :], in_=b_sb[t][:].indirect(l4[:]))
            else:
                nc.scalar.activation(out=b_pick[:, t, :], in_=b_sb[t][:].indirect(l4[:]), func=COPY)

        hid = sb("hid", PACK * O, BF16)
        nc.vector.tensor_tensor(
            out=hid[:].rearrange("p (g i t) -> p g t i", t=PACK, i=4),
            in0=b_pick[:].rearrange("p t (g i) -> p g t i", i=4),
            in1=gate[:].rearrange("p t (g i) -> p g t i", i=4),
            op=MULT,
        )
        hid_w, hid_s = sb("hid_w", O, U32), sb("hid_s", O, U8)
        nc.vector.quantize_mx(out=hid_w[:].bitcast(E5M2X4), scales=hid_s[:], in_=hid[:])

        last = sb("last", 2 * O, F32, tag="b_sb2")
        for h in range(2):
            nc.scalar.activation(out=last[:, h * O : (h + 1) * O], in_=tz_t[h][:].indirect(l5[:]), func=SIGMOID,
                                 bias=bo_t[:, h : h + 1], scale=so_t[:, h : h + 1])
            p_ps = psum.tile([P, O], F32, name="p_ps", tag="a")
            nc.tensor.matmul_mx(out=p_ps[:], lhsT=wb_w[:, 2 * h * P : 2 * (h + 1) * P].bitcast(E2M1X4),
                                lhsT_scale=wb_s[:, h * P : (h + 1) * P],
                                rhs=hid_w[:].bitcast(E5M2X4), rhs_scale=hid_s[:], start=True, stop=True)
            res = sb(f"res{h}", O, F32)
            nc.vector.tensor_tensor(out=res[:], in0=p_ps[:], in1=last[:, h * O : (h + 1) * O], op=MULT)
            queue = nc.sync if h == 0 else nc.scalar
            queue.dma_start(out=out[h * P : (h + 1) * P, :], in_=res[:])
